import numpy as np
import ml_dtypes


def mxq(x, axis, fmt="e4m3"):
    dtype, down = {"e4m3": (ml_dtypes.float8_e4m3fn, 7), "e5m2": (ml_dtypes.float8_e5m2, 14)}[fmt]
    v = np.moveaxis(np.asarray(x, np.float32).astype(ml_dtypes.bfloat16).astype(np.float64), axis, -1)
    blocks = v.reshape(v.shape[:-1] + (-1, 32))
    amax = np.abs(blocks).max(-1, keepdims=True)
    byte = np.maximum(np.where(amax > 0, np.frexp(amax)[1] - 1 + 127, 0) - down, 1)
    scale = np.exp2(byte - 127.0)
    codes = (blocks / scale).astype(np.float32).astype(dtype).astype(np.float64)
    return np.moveaxis((codes * scale).reshape(v.shape), -1, axis)


WIDE = False


def mx_kscale(k, group=512):
    if not WIDE:
        return np.ones(k)
    levels = np.array([18, -18])
    if group != 512:
        return np.exp2(np.random.permutation(np.resize(levels, k // group))).repeat(group)
    if k % 512:
        return np.exp2(np.random.permutation(np.resize(levels, k // 32))).repeat(32)
    a = np.empty((k // 512, 16))
    for p in range(k // 512):
        a[p, :8] = np.random.permutation(np.resize(levels, 8))
        for g in range(8):
            far = levels[np.abs(levels - a[p, g]) >= 10]
            a[p, g + 8] = far[np.random.randint(len(far))]
    return np.exp2(a.ravel()).repeat(32)


def f64(x):
    return np.asarray(x).astype(np.float64)


G, D, K, M, N = 4, 128, 1024, 128, 512


def setup_inputs():
    n = np.random.standard_normal
    s = mx_kscale(D, 0)[:, None]
    u = mx_kscale(K)[:, None]
    return {
        "x": (n((G, D, N)) * s).astype(np.float32),
        "w1": (n((G, D, K)) / np.sqrt(D) / s).astype(np.float32),
        "hs": (np.random.uniform(0.5, 2.0, (G, K, 1)) * u).astype(np.float32),
        "w2": (n((G, K, M)) / np.sqrt(K) / u).astype(np.float32),
        "r": n((G, M, N)).astype(np.float32),
    }


def reference(x, w1, hs, w2, r):
    xq = mxq(f64(x), 1, "e4m3")
    h = mxq(f64(w1), 1, "e4m3").transpose(0, 2, 1) @ xq
    h = (np.tanh(h)) * f64(hs)
    y = mxq(f64(w2), 1, "e4m3").transpose(0, 2, 1) @ mxq(h, 1, "e4m3")
    y = y + f64(r)
    return y

@@ -1,0 +1,255 @@
+from contextlib import ExitStack
+
+import concourse.mybir as mybir
+
+G, D, K, M, N = 4, 128, 1024, 128, 512
+FLOPS = 2 * G * D * K * N + 2 * G * K * M * N
+
+F32 = mybir.dt.float32
+BF16 = mybir.dt.bfloat16
+U32 = mybir.dt.uint32
+U8 = mybir.dt.uint8
+FP8X4 = mybir.dt.float8_e4m3fn_x4
+TANH = mybir.ActivationFunctionType.Tanh
+MULT = mybir.AluOpType.mult
+ADD = mybir.AluOpType.add
+
+P = 128
+PACK = 4
+ROWS = D // PACK
+K_PASS = P * PACK
+PASSES = K // K_PASS
+CHUNK = 128
+CHUNKS = N // CHUNK
+STEPS = PASSES * CHUNKS * G // 2
+HEAD_SPLIT = 44
+W1_AT = {2: 1, 3: 2, 5: 3}
+W1_V = {1: 0}
+W1_QUANT = 5
+W2_AT = {6: (0, 0), 8: (0, 1), 9: (1, 0), 10: (1, 1), 11: (2, 0), 12: (2, 1), 13: (3, 0), 14: (3, 1)}
+L2_AT = {
+    10: [(0, 0)],
+    11: [(1, 0)],
+    12: [(0, 1), (1, 1)],
+    13: [(2, 0), (2, 1)],
+    14: [(0, 2), (1, 2)],
+    15: [(2, 2), (3, 0), (3, 1), (3, 2)],
+}
+FIN_AT = {10: [(0, 0, 1)], 11: [(1, 0, 1)], 12: [(0, 1, 2), (1, 1, 2)], 13: [(2, 0, 2)], 14: [(0, 2, 3), (1, 2, 3)]}
+
+
+def tile_rows_gmlp_tanh_res_kernel(tc, x, w1, hs, w2, r, out):
+    nc = tc.nc
+    with ExitStack() as ctx:
+        sb = ctx.enter_context(tc.tile_pool(name="sb", bufs=1))
+        ps = ctx.enter_context(tc.psum_pool(name="ps", bufs=1))
+        ctx.enter_context(tc.manual_schedule())
+
+        def tiles(pool, name, count, shape, dtype):
+            return [pool.tile(shape, dtype, name="%s_%d" % (name, i), align_bytes=64) for i in range(count)]
+
+        z_bank = [ps.tile([P, PACK, CHUNK], F32, name="z_%d" % g) for g in range(G)]
+        y_bank = [ps.tile([P, N], F32, name="y_%d" % g) for g in range(G)]
+
+        x_raw = [sb.tile([P, PACK, w], F32, name="xraw_%d" % i, align_bytes=64) for i, w in enumerate((128, 128, 256))]
+        w1_raw = tiles(sb, "w1raw", 2 * PASSES, [P, PACK, K_PASS // 2], F32)
+        w2_raw = tiles(sb, "w2raw", G, [P, PASSES, PACK, M], F32)
+        r_sb = sb.tile([P, G, N], F32, name="r_sb", align_bytes=64)
+        hs_sb = tiles(sb, "hssb", PASSES, [P, G, 1, 8], F32)
+        y_sb = tiles(sb, "ysb", G, [P, N], F32)
+
+        x_bf = tiles(sb, "xbf", CHUNKS, [P, CHUNK, PACK], BF16)
+        x_codes = tiles(sb, "xc", CHUNKS, [P, CHUNK], U32)
+        x_scales = tiles(sb, "xs", CHUNKS, [P, CHUNK], U8)
+        w1_bf = tiles(sb, "w1bf", PASSES, [P, PACK, P, PACK], BF16)
+        w1_codes = tiles(sb, "w1c", PASSES, [P, K_PASS], U32)
+        w1_scales = tiles(sb, "w1s", PASSES, [P, K_PASS], U8)
+        w2_bf = tiles(sb, "w2bf", G, [P, PASSES, M, PACK], BF16)
+        w2_codes = tiles(sb, "w2c", G, [P, PASSES * M], U32)
+        w2_scales = tiles(sb, "w2s", G, [P, PASSES * M], U8)
+        h_codes = tiles(sb, "hc", STEPS, [P, 2 * CHUNK], U32)
+        h_scales = tiles(sb, "hsc", STEPS, [P, 2 * CHUNK], U8)
+        act = {}
+        h_bf = {}
+
+        x_rows = x.rearrange("g (p j) n -> (g p) j n", j=PACK)
+        w1_rows = w1.rearrange("g (p j) k -> (g p) j k", j=PACK)
+        half = K_PASS // 2
+
+        def load_hs(c):
+            nc.sync.dma_start(
+                out=hs_sb[c][:, :, 0, 0:PACK],
+                in_=hs[:, K_PASS * c : K_PASS * (c + 1), :].rearrange("g (p j) o -> p g (j o)", j=PACK),
+            )
+
+        nc.sync.dma_start(out=x_raw[0][:], in_=x_rows[:, :, 0:128])
+        nc.sync.dma_start(out=w1_raw[0][:], in_=w1_rows[:, :, 0:half])
+        nc.sync.dma_start(out=w1_raw[1][:], in_=w1_rows[:, :, half : 2 * half])
+        nc.sync.dma_start(out=x_raw[1][:], in_=x_rows[:, :, 128:256])
+        nc.sync.dma_start(out=x_raw[2][:], in_=x_rows[:, :, 256:512])
+        load_hs(0)
+        nc.sync.dma_start(out=w1_raw[2][:], in_=w1_rows[:, :, 2 * half : 3 * half])
+        nc.sync.dma_start(out=w1_raw[3][:], in_=w1_rows[:, :, 3 * half : 4 * half])
+        load_hs(1)
+        for g in range(G):
+            nc.sync.dma_start(
+                out=w2_raw[g][:].rearrange("p c j m -> p c (j m)"),
+                in_=w2[g].rearrange("(c p j) m -> p c (j m)", p=P, j=PACK),
+            )
+        nc.sync.dma_start(out=r_sb[:], in_=r.rearrange("g m n -> m g n"))
+
+        warm = sb.tile([P, 8], F32, name="warm")
+        warm_out = sb.tile([P, 8], F32, name="warm_out")
+        nc.vector.memset(warm[:], 0.0)
+        nc.scalar.activation(out=warm_out[:], in_=warm[:], func=TANH)
+
+        def interleave(copy, dst, src):
+            copy(
+                out=dst.rearrange("p (a i) j -> p a j i", i=4),
+                in_=src.rearrange("p j (a i) -> p a j i", i=4),
+            )
+
+        def x_src(q):
+            if q < 2:
+                return x_raw[q][:]
+            return x_raw[2][:, :, (q - 2) * CHUNK : (q - 1) * CHUNK]
+
+        def deal_w1(copy, c, s0, s1):
+            hf = s0 // 64
+            src = w1_raw[2 * c + hf][:].rearrange("p j (s t) -> p s j t", t=PACK)
+            copy(
+                out=w1_bf[c][:, :, s0:s1, :].rearrange("p t s j -> p s j t"),
+                in_=src[:, s0 - 64 * hf : s1 - 64 * hf, :, :],
+            )
+
+        def quantize(codes, scales, src):
+            nc.vector.quantize_mx(out=codes.bitcast(FP8X4), scales=scales, in_=src)
+
+        def quantize_x(q):
+            quantize(x_codes[q][:], x_scales[q][:], x_bf[q][:].rearrange("p n j -> p (n j)"))
+
+        def quantize_w1(c, w0, w1_end):
+            flat = w1_bf[c][:].rearrange("p t s j -> p (t s j)")
+            quantize(w1_codes[c][:, w0:w1_end], w1_scales[c][:, w0:w1_end], flat[:, PACK * w0 : PACK * w1_end])
+
+        def place(step):
+            return step // (2 * CHUNKS), (step // 2) % CHUNKS, 2 * (step % 2)
+
+        def layer1(steps):
+            for t in range(PACK):
+                for step in steps:
+                    c, q, g0 = place(step)
+                    for g in (g0, g0 + 1):
+                        rows = slice(ROWS * g, ROWS * (g + 1))
+                        cols = slice(P * t, P * (t + 1))
+                        nc.tensor.matmul_mx(
+                            out=z_bank[g][:, t, :],
+                            lhsT=w1_codes[c][rows, cols].bitcast(FP8X4),
+                            lhsT_scale=w1_scales[c][rows, cols],
+                            rhs=x_codes[q][rows, :].bitcast(FP8X4),
+                            rhs_scale=x_scales[q][rows, :],
+                            start=True,
+                            stop=True,
+                        )
+
+        def tanh(step):
+            c, q, g0 = place(step)
+            act[step] = sb.tile([P, 2, CHUNK, PACK], F32, name="act", bufs=6, align_bytes=64)
+            for u in range(2):
+                nc.scalar.activation(
+                    out=act[step][:, u, :, :], in_=z_bank[g0 + u][:].rearrange("p t n -> p n t"), func=TANH
+                )
+
+        def scale(step, u0, u1):
+            c, q, g0 = place(step)
+            if u0 == 0:
+                h_bf[step] = sb.tile([P, 2, CHUNK, PACK], BF16, name="hbf", bufs=4, align_bytes=64)
+            factor = hs_sb[c][:, g0 + u0 : g0 + u1, :, 0:PACK].broadcast_to([P, u1 - u0, CHUNK, PACK])
+            nc.vector.tensor_tensor(out=h_bf[step][:, u0:u1, :, :], in0=act[step][:, u0:u1, :, :], in1=factor, op=MULT)
+
+        def quantize_h(step, u0, u1):
+            cols = slice(CHUNK * u0, CHUNK * u1)
+            quantize(
+                h_codes[step][:, cols], h_scales[step][:, cols], h_bf[step][:, u0:u1, :, :].rearrange("p u n j -> p (u n j)")
+            )
+
+        def layer2(g, q):
+            for c in range(PASSES):
+                step = 2 * (c * CHUNKS + q) + g // 2
+                cols = slice(CHUNK * (g % 2), CHUNK * (g % 2 + 1))
+                wcols = slice(M * c, M * (c + 1))
+                nc.tensor.matmul_mx(
+                    out=y_bank[g][:, CHUNK * q : CHUNK * (q + 1)],
+                    lhsT=w2_codes[g][:, wcols].bitcast(FP8X4),
+                    lhsT_scale=w2_scales[g][:, wcols],
+                    rhs=h_codes[step][:, cols].bitcast(FP8X4),
+                    rhs_scale=h_scales[step][:, cols],
+                    start=(c == 0),
+                    stop=(c == PASSES - 1),
+                )
+
+        def finish(g, q0, q1):
+            cols = slice(CHUNK * q0, CHUNK * q1)
+            nc.vector.tensor_tensor(out=y_sb[g][:, cols], in0=y_bank[g][:, cols], in1=r_sb[:, g, cols], op=ADD)
+            nc.sync.dma_start(out=out[g, :, cols], in_=y_sb[g][:, cols])
+
+        interleave(nc.vector.tensor_copy, x_bf[0][:], x_src(0))
+        quantize_x(0)
+        for hf in range(2):
+            deal_w1(nc.vector.tensor_copy, 0, 64 * hf, 64 * hf + HEAD_SPLIT)
+            deal_w1(nc.scalar.copy, 0, 64 * hf + HEAD_SPLIT, 64 * hf + 64)
+            for t in range(PACK):
+                quantize_w1(0, P * t + 64 * hf, P * t + 64 * hf + 64)
+        layer1([0, 1])
+        interleave(nc.scalar.copy, x_bf[1][:], x_src(1))
+        quantize_x(1)
+        interleave(nc.vector.tensor_copy, x_bf[2][:], x_src(2))
+        interleave(nc.vector.tensor_copy, x_bf[3][:], x_src(3))
+
+        def quantize_w2(g):
+            quantize(w2_codes[g][:], w2_scales[g][:], w2_bf[g][:].rearrange("p c m j -> p (c m j)"))
+
+        for step in range(STEPS):
+            tanh(step)
+            if step + 2 < STEPS:
+                layer1([step + 2])
+            for g, q in L2_AT.get(step, ()):
+                layer2(g, q)
+            if step in W1_AT:
+                i = W1_AT[step]
+                deal_w1(nc.scalar.copy, 1, 32 * i, 32 * (i + 1))
+            if step in W2_AT:
+                g, c = W2_AT[step]
+                interleave(nc.scalar.copy, w2_bf[g][:, c, :, :], w2_raw[g][:, c, :, :])
+            if step == 0:
+                scale(step, 0, 1)
+                quantize_x(2)
+                scale(step, 1, 2)
+                quantize_x(3)
+            elif step == STEPS - 1:
+                scale(step, 0, 1)
+                quantize_h(step - 1, 0, 2)
+                scale(step, 1, 2)
+            else:
+                scale(step, 0, 2)
+                quantize_h(step - 1, 0, 2)
+            if step in W1_V:
+                i = W1_V[step]
+                deal_w1(nc.vector.tensor_copy, 1, 32 * i, 32 * (i + 1))
+            if step == W1_QUANT:
+                quantize_w1(1, 0, K_PASS)
+            if step in W2_AT and W2_AT[step][1] == 1:
+                quantize_w2(W2_AT[step][0])
+            for g, q0, q1 in FIN_AT.get(step, ()):
+                finish(g, q0, q1)
+        layer2(0, 3)
+        layer2(1, 3)
+        quantize_h(STEPS - 1, 0, 1)
+        finish(3, 0, 3)
+        quantize_h(STEPS - 1, 1, 2)
+        layer2(2, 3)
+        layer2(3, 3)
+        finish(0, 3, 4)
+        finish(1, 3, 4)
+        finish(2, 2, 4)
+        finish(3, 3, 4)

@@ -11,6 +11,7 @@ U32 = mybir.dt.uint32
 U8 = mybir.dt.uint8
 FP8X4 = mybir.dt.float8_e4m3fn_x4
 TANH = mybir.ActivationFunctionType.Tanh
+COPY = mybir.ActivationFunctionType.Copy
 MULT = mybir.AluOpType.mult
 ADD = mybir.AluOpType.add
 
@@ -22,20 +23,19 @@ PASSES = K // K_PASS
 CHUNK = 128
 CHUNKS = N // CHUNK
 STEPS = PASSES * CHUNKS * G // 2
-HEAD_SPLIT = 44
-W1_AT = {2: 1, 3: 2, 5: 3}
-W1_V = {1: 0}
-W1_QUANT = 5
-W2_AT = {6: (0, 0), 8: (0, 1), 9: (1, 0), 10: (1, 1), 11: (2, 0), 12: (2, 1), 13: (3, 0), 14: (3, 1)}
+HEAD_SPLIT = 36
+W1_AT = {4: 3}
+W1_V = {0: 0, 1: 1, 2: 2}
+W1_QUANT = 4
+W2_AT = {6: (0, 0), 7: (0, 1), 8: (1, 0), 9: (1, 1), 11: (2, 0), 12: (2, 1), 13: (3, 0), 14: (3, 1)}
 L2_AT = {
-    10: [(0, 0)],
-    11: [(1, 0)],
-    12: [(0, 1), (1, 1)],
-    13: [(2, 0), (2, 1)],
-    14: [(0, 2), (1, 2)],
-    15: [(2, 2), (3, 0), (3, 1), (3, 2)],
+    11: [(0, 0, 2, 0, 1)],
+    12: [(1, 0, 2, 1, 2)],
+    13: [(2, 2, 3, 0, 2)],
+    14: [(0, 0, 2, 2, 3)],
+    15: [(3, 3, 4, 0, 3)],
 }
-FIN_AT = {10: [(0, 0, 1)], 11: [(1, 0, 1)], 12: [(0, 1, 2), (1, 1, 2)], 13: [(2, 0, 2)], 14: [(0, 2, 3), (1, 2, 3)]}
+FIN_AT = {12: [(0, 0, 2, 0, 1)], 13: [(1, 0, 2, 1, 2)], 14: [(0, 0, 2, 2, 3)], 15: [(2, 2, 3, 0, 2)]}
 
 
 def tile_rows_gmlp_tanh_res_kernel(tc, x, w1, hs, w2, r, out):
@@ -56,7 +56,7 @@ def tile_rows_gmlp_tanh_res_kernel(tc, x, w1, hs, w2, r, out):
         w2_raw = tiles(sb, "w2raw", G, [P, PASSES, PACK, M], F32)
         r_sb = sb.tile([P, G, N], F32, name="r_sb", align_bytes=64)
         hs_sb = tiles(sb, "hssb", PASSES, [P, G, 1, 8], F32)
-        y_sb = tiles(sb, "ysb", G, [P, N], F32)
+        y_sb = sb.tile([P, G, N], F32, name="y_sb", align_bytes=64)
 
         x_bf = tiles(sb, "xbf", CHUNKS, [P, CHUNK, PACK], BF16)
         x_codes = tiles(sb, "xc", CHUNKS, [P, CHUNK], U32)
@@ -67,10 +67,12 @@ def tile_rows_gmlp_tanh_res_kernel(tc, x, w1, hs, w2, r, out):
         w2_bf = tiles(sb, "w2bf", G, [P, PASSES, M, PACK], BF16)
         w2_codes = tiles(sb, "w2c", G, [P, PASSES * M], U32)
         w2_scales = tiles(sb, "w2s", G, [P, PASSES * M], U8)
-        h_codes = tiles(sb, "hc", STEPS, [P, 2 * CHUNK], U32)
-        h_scales = tiles(sb, "hsc", STEPS, [P, 2 * CHUNK], U8)
-        act = {}
-        h_bf = {}
+        h_codes = tiles(sb, "hc", STEPS // 2, [P, G * CHUNK], U32)
+        h_scales = tiles(sb, "hsc", STEPS // 2, [P, G * CHUNK], U8)
+        act = tiles(sb, "act", STEPS, [P, 2, CHUNK, PACK], F32)
+        h_bf = tiles(sb, "hbf", STEPS // 2, [P, G, CHUNK, PACK], BF16)
+
+        last_bf = sb.tile([P, PACK, CHUNK], BF16, name="last_bf", align_bytes=64)
 
         x_rows = x.rearrange("g (p j) n -> (g p) j n", j=PACK)
         w1_rows = w1.rearrange("g (p j) k -> (g p) j k", j=PACK)
@@ -136,10 +138,10 @@ def tile_rows_gmlp_tanh_res_kernel(tc, x, w1, hs, w2, r, out):
             return step // (2 * CHUNKS), (step // 2) % CHUNKS, 2 * (step % 2)
 
         def layer1(steps):
-            for t in range(PACK):
-                for step in steps:
-                    c, q, g0 = place(step)
-                    for g in (g0, g0 + 1):
+            for step in steps:
+                c, q, g0 = place(step)
+                for g in (g0, g0 + 1):
+                    for t in range(PACK):
                         rows = slice(ROWS * g, ROWS * (g + 1))
                         cols = slice(P * t, P * (t + 1))
                         nc.tensor.matmul_mx(
@@ -154,7 +156,6 @@ def tile_rows_gmlp_tanh_res_kernel(tc, x, w1, hs, w2, r, out):
 
         def tanh(step):
             c, q, g0 = place(step)
-            act[step] = sb.tile([P, 2, CHUNK, PACK], F32, name="act", bufs=6, align_bytes=64)
             for u in range(2):
                 nc.scalar.activation(
                     out=act[step][:, u, :, :], in_=z_bank[g0 + u][:].rearrange("p t n -> p n t"), func=TANH
@@ -162,36 +163,39 @@ def tile_rows_gmlp_tanh_res_kernel(tc, x, w1, hs, w2, r, out):
 
         def scale(step, u0, u1):
             c, q, g0 = place(step)
-            if u0 == 0:
-                h_bf[step] = sb.tile([P, 2, CHUNK, PACK], BF16, name="hbf", bufs=4, align_bytes=64)
             factor = hs_sb[c][:, g0 + u0 : g0 + u1, :, 0:PACK].broadcast_to([P, u1 - u0, CHUNK, PACK])
-            nc.vector.tensor_tensor(out=h_bf[step][:, u0:u1, :, :], in0=act[step][:, u0:u1, :, :], in1=factor, op=MULT)
+            nc.vector.tensor_tensor(out=h_bf[step // 2][:, g0 + u0 : g0 + u1, :, :], in0=act[step][:, u0:u1, :, :], in1=factor, op=MULT)
 
-        def quantize_h(step, u0, u1):
-            cols = slice(CHUNK * u0, CHUNK * u1)
+        def quantize_h(rnd, g0, g1):
+            cols = slice(CHUNK * g0, CHUNK * g1)
             quantize(
-                h_codes[step][:, cols], h_scales[step][:, cols], h_bf[step][:, u0:u1, :, :].rearrange("p u n j -> p (u n j)")
+                h_codes[rnd][:, cols], h_scales[rnd][:, cols], h_bf[rnd][:, g0:g1, :, :].rearrange("p u n j -> p (u n j)")
             )
 
-        def layer2(g, q):
-            for c in range(PASSES):
-                step = 2 * (c * CHUNKS + q) + g // 2
-                cols = slice(CHUNK * (g % 2), CHUNK * (g % 2 + 1))
-                wcols = slice(M * c, M * (c + 1))
-                nc.tensor.matmul_mx(
-                    out=y_bank[g][:, CHUNK * q : CHUNK * (q + 1)],
-                    lhsT=w2_codes[g][:, wcols].bitcast(FP8X4),
-                    lhsT_scale=w2_scales[g][:, wcols],
-                    rhs=h_codes[step][:, cols].bitcast(FP8X4),
-                    rhs_scale=h_scales[step][:, cols],
-                    start=(c == 0),
-                    stop=(c == PASSES - 1),
-                )
+        def layer2(bank, g0, g1, q0, q1):
+            for g in range(g0, g1):
+                for q in range(q0, q1):
+                    slot = (g - g0) * (q1 - q0) + q - q0
+                    for c in range(PASSES):
+                        rnd = c * CHUNKS + q
+                        cols = slice(CHUNK * g, CHUNK * (g + 1))
+                        wcols = slice(M * c, M * (c + 1))
+                        nc.tensor.matmul_mx(
+                            out=y_bank[bank][:, CHUNK * slot : CHUNK * (slot + 1)],
+                            lhsT=w2_codes[g][:, wcols].bitcast(FP8X4),
+                            lhsT_scale=w2_scales[g][:, wcols],
+                            rhs=h_codes[rnd][:, cols].bitcast(FP8X4),
+                            rhs_scale=h_scales[rnd][:, cols],
+                            start=(c == 0),
+                            stop=(c == PASSES - 1),
+                        )
 
-        def finish(g, q0, q1):
+        def finish(bank, g0, g1, q0, q1):
             cols = slice(CHUNK * q0, CHUNK * q1)
-            nc.vector.tensor_tensor(out=y_sb[g][:, cols], in0=y_bank[g][:, cols], in1=r_sb[:, g, cols], op=ADD)
-            nc.sync.dma_start(out=out[g, :, cols], in_=y_sb[g][:, cols])
+            width = CHUNK * (q1 - q0)
+            sums = y_bank[bank][:, 0 : (g1 - g0) * width].rearrange("m (g n) -> m g n", n=width)
+            nc.vector.tensor_tensor(out=y_sb[:, g0:g1, cols], in0=sums, in1=r_sb[:, g0:g1, cols], op=ADD)
+            nc.sync.dma_start(out=out[g0:g1, :, cols].rearrange("g m n -> m g n"), in_=y_sb[:, g0:g1, cols])
 
         interleave(nc.vector.tensor_copy, x_bf[0][:], x_src(0))
         quantize_x(0)
@@ -210,11 +214,25 @@ def tile_rows_gmlp_tanh_res_kernel(tc, x, w1, hs, w2, r, out):
             quantize(w2_codes[g][:], w2_scales[g][:], w2_bf[g][:].rearrange("p c m j -> p (c m j)"))
 
         for step in range(STEPS):
-            tanh(step)
+            rnd, g0 = step // 2, 2 * (step % 2)
+            last_rnd, last_g0 = (step - 1) // 2, 2 * ((step - 1) % 2)
+            if step < STEPS - 1:
+                tanh(step)
+            else:
+                plain = act[step][:, 1, :, :].rearrange("p n t -> p (n t)").rearrange("p (t n) -> p t n", t=PACK)
+                nc.scalar.activation(out=plain, in_=z_bank[3][:], func=TANH)
+                nc.scalar.activation(
+                    out=act[step][:, 0, :, :], in_=z_bank[2][:].rearrange("p t n -> p n t"), func=TANH
+                )
+                for t in range(PACK):
+                    nc.scalar.activation(
+                        out=last_bf[:, t, :], in_=plain[:, t, :], func=COPY, scale=hs_sb[1][:, 3, 0, t : t + 1]
+                    )
+                interleave(nc.scalar.copy, h_bf[rnd][:, 3, :, :], last_bf[:])
             if step + 2 < STEPS:
                 layer1([step + 2])
-            for g, q in L2_AT.get(step, ()):
-                layer2(g, q)
+            for block in L2_AT.get(step, ()):
+                layer2(*block)
             if step in W1_AT:
                 i = W1_AT[step]
                 deal_w1(nc.scalar.copy, 1, 32 * i, 32 * (i + 1))
@@ -224,15 +242,17 @@ def tile_rows_gmlp_tanh_res_kernel(tc, x, w1, hs, w2, r, out):
             if step == 0:
                 scale(step, 0, 1)
                 quantize_x(2)
-                scale(step, 1, 2)
                 quantize_x(3)
+                scale(step, 1, 2)
             elif step == STEPS - 1:
                 scale(step, 0, 1)
-                quantize_h(step - 1, 0, 2)
-                scale(step, 1, 2)
+                quantize_h(last_rnd, last_g0, last_g0 + 2)
             else:
                 scale(step, 0, 2)
-                quantize_h(step - 1, 0, 2)
+                if step > STEPS // 2:
+                    quantize_h(last_rnd, last_g0, last_g0 + 2)
+                elif step % 2 == 0:
+                    quantize_h(last_rnd, 0, G)
             if step in W1_V:
                 i = W1_V[step]
                 deal_w1(nc.vector.tensor_copy, 1, 32 * i, 32 * (i + 1))
@@ -240,16 +260,14 @@ def tile_rows_gmlp_tanh_res_kernel(tc, x, w1, hs, w2, r, out):
                 quantize_w1(1, 0, K_PASS)
             if step in W2_AT and W2_AT[step][1] == 1:
                 quantize_w2(W2_AT[step][0])
-            for g, q0, q1 in FIN_AT.get(step, ()):
-                finish(g, q0, q1)
-        layer2(0, 3)
-        layer2(1, 3)
-        quantize_h(STEPS - 1, 0, 1)
-        finish(3, 0, 3)
-        quantize_h(STEPS - 1, 1, 2)
-        layer2(2, 3)
-        layer2(3, 3)
-        finish(0, 3, 4)
-        finish(1, 3, 4)
-        finish(2, 2, 4)
-        finish(3, 3, 4)
+            for block in FIN_AT.get(step, ()):
+                finish(*block)
+        layer2(0, 0, 2, 3, 4)
+        quantize_h(7, 2, 3)
+        finish(3, 3, 4, 0, 3)
+        quantize_h(7, 3, 4)
+        layer2(1, 2, 3, 2, 4)
+        layer2(2, 3, 4, 3, 4)
+        finish(0, 0, 2, 3, 4)
+        finish(1, 2, 3, 2, 4)
+        finish(2, 3, 4, 3, 4)

@@ -24,18 +24,12 @@ CHUNK = 128
 CHUNKS = N // CHUNK
 STEPS = PASSES * CHUNKS * G // 2
 HEAD_SPLIT = 36
-W1_AT = {4: 3}
-W1_V = {0: 0, 1: 1, 2: 2}
+W1_AT = {3: 2, 4: 3}
+W1_V = {0: 0, 2: 1}
 W1_QUANT = 4
-W2_AT = {6: (0, 0), 7: (0, 1), 8: (1, 0), 9: (1, 1), 11: (2, 0), 12: (2, 1), 13: (3, 0), 14: (3, 1)}
-L2_AT = {
-    11: [(0, 0, 2, 0, 1)],
-    12: [(1, 0, 2, 1, 2)],
-    13: [(2, 2, 3, 0, 2)],
-    14: [(0, 0, 2, 2, 3)],
-    15: [(3, 3, 4, 0, 3)],
-}
-FIN_AT = {12: [(0, 0, 2, 0, 1)], 13: [(1, 0, 2, 1, 2)], 14: [(0, 0, 2, 2, 3)], 15: [(2, 2, 3, 0, 2)]}
+W2_STEPS = (6, 8, 9, 10, 12, 13, 14, 14)
+L2_AT = {12: [(0, 0, 2, 0, 2)], 14: [(1, 0, 2, 2, 3)], 15: [(2, 2, 3, 0, 3), (3, 3, 4, 0, 3)]}
+FIN_AT = {13: [(0, 0, 2, 0, 2)], 14: [(1, 0, 2, 2, 3)], 15: [(2, 2, 3, 0, 3)]}
 
 
 def tile_rows_gmlp_tanh_res_kernel(tc, x, w1, hs, w2, r, out):
@@ -100,10 +94,8 @@ def tile_rows_gmlp_tanh_res_kernel(tc, x, w1, hs, w2, r, out):
             )
         nc.sync.dma_start(out=r_sb[:], in_=r.rearrange("g m n -> m g n"))
 
-        warm = sb.tile([P, 8], F32, name="warm")
-        warm_out = sb.tile([P, 8], F32, name="warm_out")
-        nc.vector.memset(warm[:], 0.0)
-        nc.scalar.activation(out=warm_out[:], in_=warm[:], func=TANH)
+        def scalar_cast(out, in_):
+            nc.scalar.activation(out=out, in_=in_, func=COPY)
 
         def interleave(copy, dst, src):
             copy(
@@ -201,7 +193,7 @@ def tile_rows_gmlp_tanh_res_kernel(tc, x, w1, hs, w2, r, out):
         quantize_x(0)
         for hf in range(2):
             deal_w1(nc.vector.tensor_copy, 0, 64 * hf, 64 * hf + HEAD_SPLIT)
-            deal_w1(nc.scalar.copy, 0, 64 * hf + HEAD_SPLIT, 64 * hf + 64)
+            deal_w1(scalar_cast, 0, 64 * hf + HEAD_SPLIT, 64 * hf + 64)
             for t in range(PACK):
                 quantize_w1(0, P * t + 64 * hf, P * t + 64 * hf + 64)
         layer1([0, 1])
@@ -236,9 +228,10 @@ def tile_rows_gmlp_tanh_res_kernel(tc, x, w1, hs, w2, r, out):
             if step in W1_AT:
                 i = W1_AT[step]
                 deal_w1(nc.scalar.copy, 1, 32 * i, 32 * (i + 1))
-            if step in W2_AT:
-                g, c = W2_AT[step]
-                interleave(nc.scalar.copy, w2_bf[g][:, c, :, :], w2_raw[g][:, c, :, :])
+            for i, at in enumerate(W2_STEPS):
+                if at == step:
+                    g, c = divmod(i, PASSES)
+                    interleave(nc.scalar.copy, w2_bf[g][:, c, :, :], w2_raw[g][:, c, :, :])
             if step == 0:
                 scale(step, 0, 1)
                 quantize_x(2)
@@ -258,16 +251,17 @@ def tile_rows_gmlp_tanh_res_kernel(tc, x, w1, hs, w2, r, out):
                 deal_w1(nc.vector.tensor_copy, 1, 32 * i, 32 * (i + 1))
             if step == W1_QUANT:
                 quantize_w1(1, 0, K_PASS)
-            if step in W2_AT and W2_AT[step][1] == 1:
-                quantize_w2(W2_AT[step][0])
+            for g in range(G):
+                if W2_STEPS[PASSES * g + 1] == step:
+                    quantize_w2(g)
             for block in FIN_AT.get(step, ()):
                 finish(*block)
         layer2(0, 0, 2, 3, 4)
         quantize_h(7, 2, 3)
         finish(3, 3, 4, 0, 3)
         quantize_h(7, 3, 4)
-        layer2(1, 2, 3, 2, 4)
+        layer2(1, 2, 3, 3, 4)
         layer2(2, 3, 4, 3, 4)
         finish(0, 0, 2, 3, 4)
-        finish(1, 2, 3, 2, 4)
+        finish(1, 2, 3, 3, 4)
         finish(2, 3, 4, 3, 4)

from contextlib import ExitStack

import concourse.mybir as mybir

G, D, K, M, N = 4, 128, 1024, 128, 512
FLOPS = 2 * G * D * K * N + 2 * G * K * M * N

F32 = mybir.dt.float32
BF16 = mybir.dt.bfloat16
U32 = mybir.dt.uint32
U8 = mybir.dt.uint8
FP8X4 = mybir.dt.float8_e4m3fn_x4
TANH = mybir.ActivationFunctionType.Tanh
COPY = mybir.ActivationFunctionType.Copy
MULT = mybir.AluOpType.mult
ADD = mybir.AluOpType.add

P = 128
PACK = 4
ROWS = D // PACK
K_PASS = P * PACK
PASSES = K // K_PASS
CHUNK = 128
CHUNKS = N // CHUNK
STEPS = PASSES * CHUNKS * G // 2
HEAD_SPLIT = 36
W1_AT = {3: 2, 4: 3}
W1_V = {0: 0, 2: 1}
W1_QUANT = 4
W2_STEPS = (6, 8, 9, 10, 12, 13, 14, 14)
L2_AT = {12: [(0, 0, 2, 0, 2)], 14: [(1, 0, 2, 2, 3)], 15: [(2, 2, 3, 0, 3), (3, 3, 4, 0, 3)]}
FIN_AT = {13: [(0, 0, 2, 0, 2)], 14: [(1, 0, 2, 2, 3)], 15: [(2, 2, 3, 0, 3)]}


def tile_rows_gmlp_tanh_res_kernel(tc, x, w1, hs, w2, r, out):
    nc = tc.nc
    with ExitStack() as ctx:
        sb = ctx.enter_context(tc.tile_pool(name="sb", bufs=1))
        ps = ctx.enter_context(tc.psum_pool(name="ps", bufs=1))
        ctx.enter_context(tc.manual_schedule())

        def tiles(pool, name, count, shape, dtype):
            return [pool.tile(shape, dtype, name="%s_%d" % (name, i), align_bytes=64) for i in range(count)]

        z_bank = [ps.tile([P, PACK, CHUNK], F32, name="z_%d" % g) for g in range(G)]
        y_bank = [ps.tile([P, N], F32, name="y_%d" % g) for g in range(G)]

        x_raw = [sb.tile([P, PACK, w], F32, name="xraw_%d" % i, align_bytes=64) for i, w in enumerate((128, 128, 256))]
        w1_raw = tiles(sb, "w1raw", 2 * PASSES, [P, PACK, K_PASS // 2], F32)
        w2_raw = tiles(sb, "w2raw", G, [P, PASSES, PACK, M], F32)
        r_sb = sb.tile([P, G, N], F32, name="r_sb", align_bytes=64)
        hs_sb = tiles(sb, "hssb", PASSES, [P, G, 1, 8], F32)
        y_sb = sb.tile([P, G, N], F32, name="y_sb", align_bytes=64)

        x_bf = tiles(sb, "xbf", CHUNKS, [P, CHUNK, PACK], BF16)
        x_codes = tiles(sb, "xc", CHUNKS, [P, CHUNK], U32)
        x_scales = tiles(sb, "xs", CHUNKS, [P, CHUNK], U8)
        w1_bf = tiles(sb, "w1bf", PASSES, [P, PACK, P, PACK], BF16)
        w1_codes = tiles(sb, "w1c", PASSES, [P, K_PASS], U32)
        w1_scales = tiles(sb, "w1s", PASSES, [P, K_PASS], U8)
        w2_bf = tiles(sb, "w2bf", G, [P, PASSES, M, PACK], BF16)
        w2_codes = tiles(sb, "w2c", G, [P, PASSES * M], U32)
        w2_scales = tiles(sb, "w2s", G, [P, PASSES * M], U8)
        h_codes = tiles(sb, "hc", STEPS // 2, [P, G * CHUNK], U32)
        h_scales = tiles(sb, "hsc", STEPS // 2, [P, G * CHUNK], U8)
        act = tiles(sb, "act", STEPS, [P, 2, CHUNK, PACK], F32)
        h_bf = tiles(sb, "hbf", STEPS // 2, [P, G, CHUNK, PACK], BF16)

        last_bf = sb.tile([P, PACK, CHUNK], BF16, name="last_bf", align_bytes=64)

        x_rows = x.rearrange("g (p j) n -> (g p) j n", j=PACK)
        w1_rows = w1.rearrange("g (p j) k -> (g p) j k", j=PACK)
        half = K_PASS // 2

        def load_hs(c):
            nc.sync.dma_start(
                out=hs_sb[c][:, :, 0, 0:PACK],
                in_=hs[:, K_PASS * c : K_PASS * (c + 1), :].rearrange("g (p j) o -> p g (j o)", j=PACK),
            )

        nc.sync.dma_start(out=x_raw[0][:], in_=x_rows[:, :, 0:128])
        nc.sync.dma_start(out=w1_raw[0][:], in_=w1_rows[:, :, 0:half])
        nc.sync.dma_start(out=w1_raw[1][:], in_=w1_rows[:, :, half : 2 * half])
        nc.sync.dma_start(out=x_raw[1][:], in_=x_rows[:, :, 128:256])
        nc.sync.dma_start(out=x_raw[2][:], in_=x_rows[:, :, 256:512])
        load_hs(0)
        nc.sync.dma_start(out=w1_raw[2][:], in_=w1_rows[:, :, 2 * half : 3 * half])
        nc.sync.dma_start(out=w1_raw[3][:], in_=w1_rows[:, :, 3 * half : 4 * half])
        load_hs(1)
        for g in range(G):
            nc.sync.dma_start(
                out=w2_raw[g][:].rearrange("p c j m -> p c (j m)"),
                in_=w2[g].rearrange("(c p j) m -> p c (j m)", p=P, j=PACK),
            )
        nc.sync.dma_start(out=r_sb[:], in_=r.rearrange("g m n -> m g n"))

        def scalar_cast(out, in_):
            nc.scalar.activation(out=out, in_=in_, func=COPY)

        def interleave(copy, dst, src):
            copy(
                out=dst.rearrange("p (a i) j -> p a j i", i=4),
                in_=src.rearrange("p j (a i) -> p a j i", i=4),
            )

        def x_src(q):
            if q < 2:
                return x_raw[q][:]
            return x_raw[2][:, :, (q - 2) * CHUNK : (q - 1) * CHUNK]

        def deal_w1(copy, c, s0, s1):
            hf = s0 // 64
            src = w1_raw[2 * c + hf][:].rearrange("p j (s t) -> p s j t", t=PACK)
            copy(
                out=w1_bf[c][:, :, s0:s1, :].rearrange("p t s j -> p s j t"),
                in_=src[:, s0 - 64 * hf : s1 - 64 * hf, :, :],
            )

        def quantize(codes, scales, src):
            nc.vector.quantize_mx(out=codes.bitcast(FP8X4), scales=scales, in_=src)

        def quantize_x(q):
            quantize(x_codes[q][:], x_scales[q][:], x_bf[q][:].rearrange("p n j -> p (n j)"))

        def quantize_w1(c, w0, w1_end):
            flat = w1_bf[c][:].rearrange("p t s j -> p (t s j)")
            quantize(w1_codes[c][:, w0:w1_end], w1_scales[c][:, w0:w1_end], flat[:, PACK * w0 : PACK * w1_end])

        def place(step):
            return step // (2 * CHUNKS), (step // 2) % CHUNKS, 2 * (step % 2)

        def layer1(steps):
            for step in steps:
                c, q, g0 = place(step)
                for g in (g0, g0 + 1):
                    for t in range(PACK):
                        rows = slice(ROWS * g, ROWS * (g + 1))
                        cols = slice(P * t, P * (t + 1))
                        nc.tensor.matmul_mx(
                            out=z_bank[g][:, t, :],
                            lhsT=w1_codes[c][rows, cols].bitcast(FP8X4),
                            lhsT_scale=w1_scales[c][rows, cols],
                            rhs=x_codes[q][rows, :].bitcast(FP8X4),
                            rhs_scale=x_scales[q][rows, :],
                            start=True,
                            stop=True,
                        )

        def tanh(step):
            c, q, g0 = place(step)
            for u in range(2):
                nc.scalar.activation(
                    out=act[step][:, u, :, :], in_=z_bank[g0 + u][:].rearrange("p t n -> p n t"), func=TANH
                )

        def scale(step, u0, u1):
            c, q, g0 = place(step)
            factor = hs_sb[c][:, g0 + u0 : g0 + u1, :, 0:PACK].broadcast_to([P, u1 - u0, CHUNK, PACK])
            nc.vector.tensor_tensor(out=h_bf[step // 2][:, g0 + u0 : g0 + u1, :, :], in0=act[step][:, u0:u1, :, :], in1=factor, op=MULT)

        def quantize_h(rnd, g0, g1):
            cols = slice(CHUNK * g0, CHUNK * g1)
            quantize(
                h_codes[rnd][:, cols], h_scales[rnd][:, cols], h_bf[rnd][:, g0:g1, :, :].rearrange("p u n j -> p (u n j)")
            )

        def layer2(bank, g0, g1, q0, q1):
            for g in range(g0, g1):
                for q in range(q0, q1):
                    slot = (g - g0) * (q1 - q0) + q - q0
                    for c in range(PASSES):
                        rnd = c * CHUNKS + q
                        cols = slice(CHUNK * g, CHUNK * (g + 1))
                        wcols = slice(M * c, M * (c + 1))
                        nc.tensor.matmul_mx(
                            out=y_bank[bank][:, CHUNK * slot : CHUNK * (slot + 1)],
                            lhsT=w2_codes[g][:, wcols].bitcast(FP8X4),
                            lhsT_scale=w2_scales[g][:, wcols],
                            rhs=h_codes[rnd][:, cols].bitcast(FP8X4),
                            rhs_scale=h_scales[rnd][:, cols],
                            start=(c == 0),
                            stop=(c == PASSES - 1),
                        )

        def finish(bank, g0, g1, q0, q1):
            cols = slice(CHUNK * q0, CHUNK * q1)
            width = CHUNK * (q1 - q0)
            sums = y_bank[bank][:, 0 : (g1 - g0) * width].rearrange("m (g n) -> m g n", n=width)
            nc.vector.tensor_tensor(out=y_sb[:, g0:g1, cols], in0=sums, in1=r_sb[:, g0:g1, cols], op=ADD)
            nc.sync.dma_start(out=out[g0:g1, :, cols].rearrange("g m n -> m g n"), in_=y_sb[:, g0:g1, cols])

        interleave(nc.vector.tensor_copy, x_bf[0][:], x_src(0))
        quantize_x(0)
        for hf in range(2):
            deal_w1(nc.vector.tensor_copy, 0, 64 * hf, 64 * hf + HEAD_SPLIT)
            deal_w1(scalar_cast, 0, 64 * hf + HEAD_SPLIT, 64 * hf + 64)
            for t in range(PACK):
                quantize_w1(0, P * t + 64 * hf, P * t + 64 * hf + 64)
        layer1([0, 1])
        interleave(nc.scalar.copy, x_bf[1][:], x_src(1))
        quantize_x(1)
        interleave(nc.vector.tensor_copy, x_bf[2][:], x_src(2))
        interleave(nc.vector.tensor_copy, x_bf[3][:], x_src(3))

        def quantize_w2(g):
            quantize(w2_codes[g][:], w2_scales[g][:], w2_bf[g][:].rearrange("p c m j -> p (c m j)"))

        for step in range(STEPS):
            rnd, g0 = step // 2, 2 * (step % 2)
            last_rnd, last_g0 = (step - 1) // 2, 2 * ((step - 1) % 2)
            if step < STEPS - 1:
                tanh(step)
            else:
                plain = act[step][:, 1, :, :].rearrange("p n t -> p (n t)").rearrange("p (t n) -> p t n", t=PACK)
                nc.scalar.activation(out=plain, in_=z_bank[3][:], func=TANH)
                nc.scalar.activation(
                    out=act[step][:, 0, :, :], in_=z_bank[2][:].rearrange("p t n -> p n t"), func=TANH
                )
                for t in range(PACK):
                    nc.scalar.activation(
                        out=last_bf[:, t, :], in_=plain[:, t, :], func=COPY, scale=hs_sb[1][:, 3, 0, t : t + 1]
                    )
                interleave(nc.scalar.copy, h_bf[rnd][:, 3, :, :], last_bf[:])
            if step + 2 < STEPS:
                layer1([step + 2])
            for block in L2_AT.get(step, ()):
                layer2(*block)
            if step in W1_AT:
                i = W1_AT[step]
                deal_w1(nc.scalar.copy, 1, 32 * i, 32 * (i + 1))
            for i, at in enumerate(W2_STEPS):
                if at == step:
                    g, c = divmod(i, PASSES)
                    interleave(nc.scalar.copy, w2_bf[g][:, c, :, :], w2_raw[g][:, c, :, :])
            if step == 0:
                scale(step, 0, 1)
                quantize_x(2)
                quantize_x(3)
                scale(step, 1, 2)
            elif step == STEPS - 1:
                scale(step, 0, 1)
                quantize_h(last_rnd, last_g0, last_g0 + 2)
            else:
                scale(step, 0, 2)
                if step > STEPS // 2:
                    quantize_h(last_rnd, last_g0, last_g0 + 2)
                elif step % 2 == 0:
                    quantize_h(last_rnd, 0, G)
            if step in W1_V:
                i = W1_V[step]
                deal_w1(nc.vector.tensor_copy, 1, 32 * i, 32 * (i + 1))
            if step == W1_QUANT:
                quantize_w1(1, 0, K_PASS)
            for g in range(G):
                if W2_STEPS[PASSES * g + 1] == step:
                    quantize_w2(g)
            for block in FIN_AT.get(step, ()):
                finish(*block)
        layer2(0, 0, 2, 3, 4)
        quantize_h(7, 2, 3)
        finish(3, 3, 4, 0, 3)
        quantize_h(7, 3, 4)
        layer2(1, 2, 3, 3, 4)
        layer2(2, 3, 4, 3, 4)
        finish(0, 0, 2, 3, 4)
        finish(1, 2, 3, 3, 4)
        finish(2, 3, 4, 3, 4)
